import numpy as np
import ml_dtypes


def mxq(x, axis, fmt="e4m3"):
    dtype, down = {"e4m3": (ml_dtypes.float8_e4m3fn, 7), "e5m2": (ml_dtypes.float8_e5m2, 14)}[fmt]
    v = np.moveaxis(np.asarray(x, np.float32).astype(ml_dtypes.bfloat16).astype(np.float64), axis, -1)
    blocks = v.reshape(v.shape[:-1] + (-1, 32))
    amax = np.abs(blocks).max(-1, keepdims=True)
    byte = np.maximum(np.where(amax > 0, np.frexp(amax)[1] - 1 + 127, 0) - down, 1)
    scale = np.exp2(byte - 127.0)
    codes = (blocks / scale).astype(np.float32).astype(dtype).astype(np.float64)
    return np.moveaxis((codes * scale).reshape(v.shape), -1, axis)


WIDE = False


def mx_kscale(k):
    if not WIDE:
        return np.ones(k)
    levels = np.array([10, -10, 5, -5, 0])
    if k % 512:
        return np.exp2(np.random.permutation(np.resize(levels, k // 32))).repeat(32)
    a = np.empty((k // 512, 16))
    for p in range(k // 512):
        a[p, :8] = np.random.permutation(np.resize(levels, 8))
        for g in range(8):
            far = levels[np.abs(levels - a[p, g]) >= 10]
            a[p, g + 8] = far[np.random.randint(len(far))]
    return np.exp2(a.ravel()).repeat(32)


def f64(x):
    return np.asarray(x).astype(np.float64)


def striped(idx):
    return np.tile(idx.reshape(-1, 16).T, (8, 1)).astype(np.uint16)


def unstriped(offs):
    return offs[:16].T.reshape(-1).astype(np.int64)


E2M1 = np.array([0.0, 0.5, 1.0, 1.5, 2.0, 3.0, 4.0, 6.0, -0.0, -0.5, -1.0, -1.5, -2.0, -3.0, -4.0, -6.0])


def pack_weight(w, fmt):
    k, n = w.shape
    w = f64(np.asarray(w, np.float32).astype(ml_dtypes.bfloat16)).reshape(k // 32, 32, n)
    amax = np.abs(w).max(1)
    if fmt == "e4m3":
        byte = np.frexp(amax)[1] - 1 + 127 - 7
    else:
        mant, ex = np.frexp(amax / 6.0)
        byte = np.where(mant > 0.5, ex, ex - 1) + 127
    byte = np.clip(np.where(amax > 0, byte, 1), 1, 254)
    scaled = (w * np.exp2(127.0 - byte)[:, None, :]).reshape(k, n).astype(np.float32)
    by_word = np.ascontiguousarray(scaled.reshape(k // 512, 128, 4, n).transpose(0, 1, 3, 2))
    if fmt == "e4m3":
        words = by_word.astype(ml_dtypes.float8_e4m3fn).view(np.uint8)
    else:
        c = by_word.astype(ml_dtypes.float4_e2m1fn).view(np.uint8) & 0xF
        words = (c[..., 0::2] | (c[..., 1::2] << 4)).reshape(k // 512, 128, 2 * n)
    return np.ascontiguousarray(words), np.ascontiguousarray(byte.astype(np.uint8).reshape(k // 512, 16, n))


def unpack_weight(words, scales, fmt):
    g, _, n = scales.shape
    words = np.ascontiguousarray(words).reshape(g, 128, n, -1)
    if fmt == "e4m3":
        vals = words.view(ml_dtypes.float8_e4m3fn).astype(np.float64)
    else:
        nib = np.empty((g, 128, n, 4), np.uint8)
        nib[..., 0::2] = words & 0xF
        nib[..., 1::2] = words >> 4
        vals = E2M1[nib]
    vals = vals * np.repeat(np.exp2(scales.astype(np.float64) - 127.0), 8, axis=1)[..., None]
    return vals.transpose(0, 1, 3, 2).reshape(g * 512, n)


def gelu(v):
    return 0.5 * v * (1.0 + np.tanh(np.sqrt(2.0 / np.pi) * (v + 0.044715 * v**3)))


K, M, T, S = 1024, 256, 2048, 1024


def setup_inputs():
    n = np.random.standard_normal
    s = mx_kscale(K)[:, None]
    w = n((K, M)) / np.sqrt(K) / s
    v = pack_weight(n((K, T)) * s, "e4m3")
    p_w4 = pack_weight(w[512:], "e2m1")
    return {
        "tab_words": v[0],
        "tab_scales": v[1],
        "w8": (w[:512]).astype(np.float32),
        "w4_words": p_w4[0],
        "w4_scales": p_w4[1],
        "gT": n((M, T)).astype(np.float32),
        "b": (0.3 * n(256)).astype(np.float32),
        "offs": striped(np.random.permutation(T)[:S]),
    }


def reference(tab_words, tab_scales, w8, w4_words, w4_scales, gT, b, offs):
    tab_ = unpack_weight(tab_words, tab_scales, "e4m3")[:, unstriped(offs)]
    w8_ = mxq(f64(w8), 0, "e4m3")
    w4_ = unpack_weight(w4_words, w4_scales, "e2m1")
    y = w8_.T @ tab_[:512] + w4_.T @ tab_[512:]
    return (gelu(y + f64(b)[:, None])) * f64(gT)[:, unstriped(offs)]

@@ -1,0 +1,114 @@
+from contextlib import ExitStack
+
+import concourse.mybir as mybir
+
+K, M, T, S = 1024, 256, 2048, 1024
+FLOPS = 2 * K * M * S
+
+F32 = mybir.dt.float32
+BF16 = mybir.dt.bfloat16
+I32 = mybir.dt.int32
+U32 = mybir.dt.uint32
+U16 = mybir.dt.uint16
+U8 = mybir.dt.uint8
+FP8X4 = mybir.dt.float8_e4m3fn_x4
+FP4X4 = mybir.dt.float4_e2m1fn_x4
+GELU = mybir.ActivationFunctionType.Gelu_apprx_tanh
+MULT = mybir.AluOpType.mult
+
+P = 128
+N_TILE = 512
+
+
+def tile_list_tabgate_gelu_kernel(tc, tab_words, tab_scales, w8, w4_words, w4_scales, gT, b, offs, out):
+    nc = tc.nc
+    with ExitStack() as ctx:
+        keep = ctx.enter_context(tc.tile_pool(name="keep", bufs=1))
+        psum = ctx.enter_context(tc.psum_pool(name="psum", bufs=1))
+
+        offsets = keep.tile([P, S // 16], U16, name="offsets")
+        nc.sync.dma_start(offsets[:], offs)
+
+        def listed(j0, j1):
+            return offsets[:, j0 // 16 : j1 // 16]
+
+        scale_win = keep.tile([P, T], U8, name="scale_win", align_bytes=64)
+        nc.vector.memset(scale_win[:].bitcast(I32), 0)
+        first_row = (4, 0)
+        for a in (1, 0):
+            for q in range(4):
+                p0 = 32 * q + first_row[a]
+                nc.scalar.dma_start(out=scale_win[p0 : p0 + 4, :].bitcast(I32), in_=tab_scales[a, 4 * q : 4 * q + 4, :].bitcast(I32))
+
+        word_win = [keep.tile([P, T], I32, name="word_win0", align_bytes=64), keep.tile([P, T], I32, name="word_win1", tag="slot_b", align_bytes=64)]
+        w8_raw = keep.tile([P, 4, M], F32, name="w8_raw", tag="slot_a", align_bytes=64)
+
+        def load_words(queue, a):
+            queue.dma_start(out=word_win[a][:], in_=tab_words[a].rearrange("p t i -> p (t i)").bitcast(I32))
+
+        load_words(nc.gpsimd, 1)
+        nc.gpsimd.dma_start(out=w8_raw[:], in_=w8.rearrange("(p i) n -> p i n", i=4))
+        load_words(nc.gpsimd, 0)
+
+        w4_plane = keep.tile([P, M], U8, name="w4_plane", align_bytes=64)
+        bias = keep.tile([P, 2], F32, name="bias")
+        nc.vector.memset(w4_plane[:].bitcast(I32), 0)
+        for q in range(4):
+            nc.scalar.dma_start(out=w4_plane[32 * q : 32 * q + 4, :].bitcast(I32), in_=w4_scales[0, 4 * q : 4 * q + 4, :].bitcast(I32))
+        w4_codes = keep.tile([P, 2 * M], U8, name="w4_codes", align_bytes=64)
+        nc.gpsimd.dma_start(out=w4_codes[:].bitcast(I32), in_=w4_words[0].bitcast(I32))
+        with nc.allow_non_contiguous_dma(reason="one bias value a partition"):
+            nc.gpsimd.dma_start(out=bias[:], in_=b.rearrange("(c p) -> p c", p=P))
+
+        plane = keep.tile([P, S], U8, name="plane", align_bytes=64)
+        codes = [[keep.tile([P, N_TILE], U32, name=f"codes{a}_{h}", align_bytes=64) for h in range(2)] for a in range(2)]
+        acc = [[psum.tile([P, N_TILE], F32, name=f"acc{c}_{h}") for h in range(2)] for c in range(2)]
+
+        nc.vector.tensor_copy(plane[:], scale_win[:].indirect(offsets[:]))
+
+        def gather_words(a, h):
+            nc.vector.tensor_copy(codes[a][h][:], word_win[a][:].bitcast(U32).indirect(listed(h * N_TILE, (h + 1) * N_TILE)))
+
+        for h in range(2):
+            gather_words(1, h)
+            for c in range(2):
+                nc.tensor.matmul_mx(
+                    out=acc[c][h][:],
+                    lhsT=w4_codes[:, 2 * c * P : 2 * (c + 1) * P].bitcast(FP4X4),
+                    lhsT_scale=w4_plane[:, c * P : (c + 1) * P],
+                    rhs=codes[1][h][:].bitcast(FP8X4),
+                    rhs_scale=plane[:, h * N_TILE : (h + 1) * N_TILE],
+                    start=True,
+                    stop=False,
+                )
+
+        w8_bf = keep.tile([P, M, 4], BF16, name="w8_bf", align_bytes=64)
+        w8_codes = keep.tile([P, M], U32, name="w8_codes", align_bytes=64)
+        w8_plane = keep.tile([P, M], U8, name="w8_plane", align_bytes=64)
+        nc.scalar.copy(out=w8_bf[:], in_=w8_raw[:].rearrange("p i n -> p n i"))
+        gate_win = [keep.tile([P, T], F32, name=f"gate_win{c}", tag=("slot_a", "slot_b")[c], align_bytes=64) for c in range(2)]
+        for c in range(2):
+            nc.sync.dma_start(out=gate_win[c][:], in_=gT[c * P : (c + 1) * P, :])
+        nc.vector.quantize_mx(out=w8_codes[:].bitcast(FP8X4), scales=w8_plane[:], in_=w8_bf[:].rearrange("p n i -> p (n i)"))
+
+        act = [[keep.tile([P, N_TILE], F32, name=f"act{c}_{h}") for h in range(2)] for c in range(2)]
+        for h in range(2):
+            gather_words(0, h)
+            for c in range(2):
+                nc.tensor.matmul_mx(
+                    out=acc[c][h][:],
+                    lhsT=w8_codes[:, c * P : (c + 1) * P].bitcast(FP8X4),
+                    lhsT_scale=w8_plane[:, c * P : (c + 1) * P],
+                    rhs=codes[0][h][:].bitcast(FP8X4),
+                    rhs_scale=plane[4:P, h * N_TILE : (h + 1) * N_TILE],
+                    start=False,
+                    stop=True,
+                )
+                nc.scalar.activation(act[c][h][:], acc[c][h][:], GELU, bias=bias[:, c : c + 1])
+
+        pieces = [(0, 0, 512), (0, 512, 1024), (1, 0, 512), (1, 512, 768), (1, 768, 1024)]
+        for c, j0, j1 in pieces:
+            h = j0 // N_TILE
+            res = keep.tile([P, j1 - j0], F32, name=f"res{c}_{j0}")
+            nc.vector.tensor_tensor(res[:], gate_win[c][:].indirect(listed(j0, j1)), act[c][h][:, j0 - h * N_TILE : j1 - h * N_TILE], MULT)
+            nc.sync.dma_start(out=out[c * P : (c + 1) * P, j0:j1], in_=res[:])

@@ -32,83 +32,108 @@ def tile_list_tabgate_gelu_kernel(tc, tab_words, tab_scales, w8, w4_words, w4_sc
         def listed(j0, j1):
             return offsets[:, j0 // 16 : j1 // 16]
 
-        scale_win = keep.tile([P, T], U8, name="scale_win", align_bytes=64)
-        nc.vector.memset(scale_win[:].bitcast(I32), 0)
-        first_row = (4, 0)
-        for a in (1, 0):
-            for q in range(4):
-                p0 = 32 * q + first_row[a]
-                nc.scalar.dma_start(out=scale_win[p0 : p0 + 4, :].bitcast(I32), in_=tab_scales[a, 4 * q : 4 * q + 4, :].bitcast(I32))
-
-        word_win = [keep.tile([P, T], I32, name="word_win0", align_bytes=64), keep.tile([P, T], I32, name="word_win1", tag="slot_b", align_bytes=64)]
-        w8_raw = keep.tile([P, 4, M], F32, name="w8_raw", tag="slot_a", align_bytes=64)
-
-        def load_words(queue, a):
-            queue.dma_start(out=word_win[a][:], in_=tab_words[a].rearrange("p t i -> p (t i)").bitcast(I32))
-
-        load_words(nc.gpsimd, 1)
-        nc.gpsimd.dma_start(out=w8_raw[:], in_=w8.rearrange("(p i) n -> p i n", i=4))
-        load_words(nc.gpsimd, 0)
-
-        w4_plane = keep.tile([P, M], U8, name="w4_plane", align_bytes=64)
-        bias = keep.tile([P, 2], F32, name="bias")
-        nc.vector.memset(w4_plane[:].bitcast(I32), 0)
+        scale_win = keep.tile([P, T], U8, name="scale_win", tag="window2", align_bytes=64)
         for q in range(4):
-            nc.scalar.dma_start(out=w4_plane[32 * q : 32 * q + 4, :].bitcast(I32), in_=w4_scales[0, 4 * q : 4 * q + 4, :].bitcast(I32))
-        w4_codes = keep.tile([P, 2 * M], U8, name="w4_codes", align_bytes=64)
-        nc.gpsimd.dma_start(out=w4_codes[:].bitcast(I32), in_=w4_words[0].bitcast(I32))
-        with nc.allow_non_contiguous_dma(reason="one bias value a partition"):
-            nc.gpsimd.dma_start(out=bias[:], in_=b.rearrange("(c p) -> p c", p=P))
+            nc.sync.dma_start(out=scale_win[32 * q + 24 : 32 * q + 32, :].bitcast(I32), in_=tab_scales[:, 4 * q : 4 * q + 4, :].bitcast(I32))
+            nc.vector.memset(scale_win[32 * q : 32 * q + 24, :].bitcast(I32), 0)
 
-        plane = keep.tile([P, S], U8, name="plane", align_bytes=64)
+        word_win = [keep.tile([P, T], I32, name=f"word_win{a}", tag=f"window{a}", align_bytes=64) for a in range(2)]
+        w8_raw = keep.tile([P, 4, M], F32, name="w8_raw")
+        w4_plane = keep.tile([P, M], U8, name="w4_plane", align_bytes=64)
+        w4_codes = keep.tile([P, 2 * M], U8, name="w4_codes", align_bytes=64)
+        bias = keep.tile([P, 2], F32, name="bias")
+
+        def load_words(a):
+            nc.sync.dma_start(out=word_win[a][:], in_=tab_words[a].rearrange("p t i -> p (t i)").bitcast(I32))
+
+        load_words(1)
+        nc.sync.dma_start(out=w8_raw[:], in_=w8.rearrange("(p i) n -> p i n", i=4))
+        for q in range(4):
+            nc.sync.dma_start(out=w4_plane[32 * q : 32 * q + 4, :].bitcast(I32), in_=w4_scales[0, 4 * q : 4 * q + 4, :].bitcast(I32))
+        load_words(0)
+        gate_win = []
+
+        nc.scalar.dma_start(out=w4_codes[:].bitcast(I32), in_=w4_words[0].bitcast(I32))
+        with nc.allow_non_contiguous_dma(reason="one bias value a partition"):
+            nc.scalar.dma_start(out=bias[:], in_=b.rearrange("(c p) -> p c", p=P))
+
+        picked = keep.tile([P, S], U8, name="picked", align_bytes=64)
+        plane = [keep.tile([P, S], U8, name=f"plane{a}", align_bytes=64) for a in range(2)]
+        nc.vector.tensor_copy(picked[:], scale_win[:].indirect(offsets[:]))
+        nc.scalar.dma_start(out=plane[1][0:100, :].bitcast(I32), in_=picked[28:128, :].bitcast(I32))
+        nc.sync.dma_start(out=plane[0][0:100, :].bitcast(I32), in_=picked[24:124, :].bitcast(I32))
+
         codes = [[keep.tile([P, N_TILE], U32, name=f"codes{a}_{h}", align_bytes=64) for h in range(2)] for a in range(2)]
         acc = [[psum.tile([P, N_TILE], F32, name=f"acc{c}_{h}") for h in range(2)] for c in range(2)]
-
-        nc.vector.tensor_copy(plane[:], scale_win[:].indirect(offsets[:]))
-
-        def gather_words(a, h):
-            nc.vector.tensor_copy(codes[a][h][:], word_win[a][:].bitcast(U32).indirect(listed(h * N_TILE, (h + 1) * N_TILE)))
-
-        for h in range(2):
-            gather_words(1, h)
-            for c in range(2):
-                nc.tensor.matmul_mx(
-                    out=acc[c][h][:],
-                    lhsT=w4_codes[:, 2 * c * P : 2 * (c + 1) * P].bitcast(FP4X4),
-                    lhsT_scale=w4_plane[:, c * P : (c + 1) * P],
-                    rhs=codes[1][h][:].bitcast(FP8X4),
-                    rhs_scale=plane[:, h * N_TILE : (h + 1) * N_TILE],
-                    start=True,
-                    stop=False,
-                )
-
+        act = [[keep.tile([P, N_TILE], F32, name=f"act{c}_{h}") for h in range(2)] for c in range(2)]
         w8_bf = keep.tile([P, M, 4], BF16, name="w8_bf", align_bytes=64)
         w8_codes = keep.tile([P, M], U32, name="w8_codes", align_bytes=64)
         w8_plane = keep.tile([P, M], U8, name="w8_plane", align_bytes=64)
-        nc.scalar.copy(out=w8_bf[:], in_=w8_raw[:].rearrange("p i n -> p n i"))
-        gate_win = [keep.tile([P, T], F32, name=f"gate_win{c}", tag=("slot_a", "slot_b")[c], align_bytes=64) for c in range(2)]
-        for c in range(2):
+
+        def gather_words(a, h, j0=0, j1=N_TILE):
+            nc.vector.tensor_copy(codes[a][h][:, j0:j1], word_win[a][:].bitcast(U32).indirect(listed(h * N_TILE + j0, h * N_TILE + j1)))
+
+        def load_gates(c, a):
+            gate_win.append(keep.tile([P, T], F32, name=f"gate_win{c}", tag=f"window{a}", align_bytes=64))
             nc.sync.dma_start(out=gate_win[c][:], in_=gT[c * P : (c + 1) * P, :])
-        nc.vector.quantize_mx(out=w8_codes[:].bitcast(FP8X4), scales=w8_plane[:], in_=w8_bf[:].rearrange("p n i -> p (n i)"))
 
-        act = [[keep.tile([P, N_TILE], F32, name=f"act{c}_{h}") for h in range(2)] for c in range(2)]
-        for h in range(2):
-            gather_words(0, h)
-            for c in range(2):
-                nc.tensor.matmul_mx(
-                    out=acc[c][h][:],
-                    lhsT=w8_codes[:, c * P : (c + 1) * P].bitcast(FP8X4),
-                    lhsT_scale=w8_plane[:, c * P : (c + 1) * P],
-                    rhs=codes[0][h][:].bitcast(FP8X4),
-                    rhs_scale=plane[4:P, h * N_TILE : (h + 1) * N_TILE],
-                    start=False,
-                    stop=True,
-                )
-                nc.scalar.activation(act[c][h][:], acc[c][h][:], GELU, bias=bias[:, c : c + 1])
+        def mm4(c, h):
+            nc.tensor.matmul_mx(
+                out=acc[c][h][:],
+                lhsT=w4_codes[:, 2 * c * P : 2 * (c + 1) * P].bitcast(FP4X4),
+                lhsT_scale=w4_plane[:, c * P : (c + 1) * P],
+                rhs=codes[1][h][:].bitcast(FP8X4),
+                rhs_scale=plane[1][:, h * N_TILE : (h + 1) * N_TILE],
+                start=True,
+                stop=False,
+            )
 
-        pieces = [(0, 0, 512), (0, 512, 1024), (1, 0, 512), (1, 512, 768), (1, 768, 1024)]
-        for c, j0, j1 in pieces:
+        def mm8(c, h, j0=0, j1=N_TILE):
+            nc.tensor.matmul_mx(
+                out=acc[c][h][:, j0:j1],
+                lhsT=w8_codes[:, c * P : (c + 1) * P].bitcast(FP8X4),
+                lhsT_scale=w8_plane[:, c * P : (c + 1) * P],
+                rhs=codes[0][h][:, j0:j1].bitcast(FP8X4),
+                rhs_scale=plane[0][:, h * N_TILE + j0 : h * N_TILE + j1],
+                start=False,
+                stop=(j1 == N_TILE),
+            )
+
+        def gelu(c, h, j0=0, j1=N_TILE):
+            nc.scalar.activation(act[c][h][:, j0:j1], acc[c][h][:, j0:j1], GELU, bias=bias[:, c : c + 1])
+
+        def cast_w8():
+            nc.scalar.copy(out=w8_bf[:], in_=w8_raw[:].rearrange("p i n -> p n i"))
+
+        def quantize_w8():
+            nc.vector.quantize_mx(out=w8_codes[:].bitcast(FP8X4), scales=w8_plane[:], in_=w8_bf[:].rearrange("p n i -> p (n i)"))
+
+        def gate(c, j0, j1):
             h = j0 // N_TILE
             res = keep.tile([P, j1 - j0], F32, name=f"res{c}_{j0}")
             nc.vector.tensor_tensor(res[:], gate_win[c][:].indirect(listed(j0, j1)), act[c][h][:, j0 - h * N_TILE : j1 - h * N_TILE], MULT)
             nc.sync.dma_start(out=out[c * P : (c + 1) * P, j0:j1], in_=res[:])
+
+        load_gates(0, 2)
+        for h in range(2):
+            gather_words(1, h)
+            mm4(0, h)
+        load_gates(1, 1)
+        cast_w8()
+        quantize_w8()
+        gather_words(0, 0)
+        mm8(0, 0)
+        gelu(0, 0)
+        for h in range(2):
+            mm4(1, h)
+        gather_words(0, 1, 0, 256)
+        mm8(0, 1, 0, 256)
+        gather_words(0, 1, 256, 512)
+        mm8(0, 1, 256, 512)
+        gelu(0, 1, 0, 256)
+        gelu(0, 1, 256, 512)
+        for h in range(2):
+            mm8(1, h)
+            gelu(1, h)
+        for c, j0, j1 in [(0, 0, 512), (0, 512, 768), (0, 768, 1024), (1, 0, 512), (1, 512, 896), (1, 896, 1024)]:
+            gate(c, j0, j1)

@@ -32,13 +32,13 @@ def tile_list_tabgate_gelu_kernel(tc, tab_words, tab_scales, w8, w4_words, w4_sc
         def listed(j0, j1):
             return offsets[:, j0 // 16 : j1 // 16]
 
-        scale_win = keep.tile([P, T], U8, name="scale_win", tag="window2", align_bytes=64)
+        scale_win = keep.tile([P, T], U8, name="scale_win", align_bytes=64)
         for q in range(4):
             nc.sync.dma_start(out=scale_win[32 * q + 24 : 32 * q + 32, :].bitcast(I32), in_=tab_scales[:, 4 * q : 4 * q + 4, :].bitcast(I32))
             nc.vector.memset(scale_win[32 * q : 32 * q + 24, :].bitcast(I32), 0)
 
         word_win = [keep.tile([P, T], I32, name=f"word_win{a}", tag=f"window{a}", align_bytes=64) for a in range(2)]
-        w8_raw = keep.tile([P, 4, M], F32, name="w8_raw")
+        w8_raw = keep.tile([P, 4, M], F32, name="w8_raw", tag="window2", align_bytes=64)
         w4_plane = keep.tile([P, M], U8, name="w4_plane", align_bytes=64)
         w4_codes = keep.tile([P, 2 * M], U8, name="w4_codes", align_bytes=64)
         bias = keep.tile([P, 2], F32, name="bias")
@@ -46,22 +46,31 @@ def tile_list_tabgate_gelu_kernel(tc, tab_words, tab_scales, w8, w4_words, w4_sc
         def load_words(a):
             nc.sync.dma_start(out=word_win[a][:], in_=tab_words[a].rearrange("p t i -> p (t i)").bitcast(I32))
 
-        load_words(1)
-        nc.sync.dma_start(out=w8_raw[:], in_=w8.rearrange("(p i) n -> p i n", i=4))
-        for q in range(4):
+        def load_w4_scales(q):
             nc.sync.dma_start(out=w4_plane[32 * q : 32 * q + 4, :].bitcast(I32), in_=w4_scales[0, 4 * q : 4 * q + 4, :].bitcast(I32))
+
+        load_words(1)
+        load_w4_scales(0)
+        load_w4_scales(1)
+        nc.sync.dma_start(out=w8_raw[:], in_=w8.rearrange("(p i) n -> p i n", i=4))
+        load_w4_scales(2)
+        load_w4_scales(3)
+        nc.sync.dma_start(out=w4_codes[:].bitcast(I32), in_=w4_words[0].bitcast(I32))
         load_words(0)
+        with nc.allow_non_contiguous_dma(reason="one bias value a partition"):
+            nc.sync.dma_start(out=bias[:], in_=b.rearrange("(c p) -> p c", p=P))
         gate_win = []
 
-        nc.scalar.dma_start(out=w4_codes[:].bitcast(I32), in_=w4_words[0].bitcast(I32))
-        with nc.allow_non_contiguous_dma(reason="one bias value a partition"):
-            nc.scalar.dma_start(out=bias[:], in_=b.rearrange("(c p) -> p c", p=P))
+        warm_in = keep.tile([P, 1], F32, name="warm_in")
+        warm_out = keep.tile([P, 1], F32, name="warm_out")
+        nc.vector.memset(warm_in[:], 0.0)
+        nc.scalar.activation(warm_out[:], warm_in[:], GELU)
 
         picked = keep.tile([P, S], U8, name="picked", align_bytes=64)
         plane = [keep.tile([P, S], U8, name=f"plane{a}", align_bytes=64) for a in range(2)]
         nc.vector.tensor_copy(picked[:], scale_win[:].indirect(offsets[:]))
         nc.scalar.dma_start(out=plane[1][0:100, :].bitcast(I32), in_=picked[28:128, :].bitcast(I32))
-        nc.sync.dma_start(out=plane[0][0:100, :].bitcast(I32), in_=picked[24:124, :].bitcast(I32))
+        nc.scalar.dma_start(out=plane[0][0:100, :].bitcast(I32), in_=picked[24:124, :].bitcast(I32))
 
         codes = [[keep.tile([P, N_TILE], U32, name=f"codes{a}_{h}", align_bytes=64) for h in range(2)] for a in range(2)]
         acc = [[psum.tile([P, N_TILE], F32, name=f"acc{c}_{h}") for h in range(2)] for c in range(2)]
@@ -103,7 +112,7 @@ def tile_list_tabgate_gelu_kernel(tc, tab_words, tab_scales, w8, w4_words, w4_sc
             nc.scalar.activation(act[c][h][:, j0:j1], acc[c][h][:, j0:j1], GELU, bias=bias[:, c : c + 1])
 
         def cast_w8():
-            nc.scalar.copy(out=w8_bf[:], in_=w8_raw[:].rearrange("p i n -> p n i"))
+            nc.vector.tensor_copy(out=w8_bf[:], in_=w8_raw[:].rearrange("p i n -> p n i"))
 
         def quantize_w8():
             nc.vector.quantize_mx(out=w8_codes[:].bitcast(FP8X4), scales=w8_plane[:], in_=w8_bf[:].rearrange("p n i -> p (n i)"))
@@ -114,12 +123,13 @@ def tile_list_tabgate_gelu_kernel(tc, tab_words, tab_scales, w8, w4_words, w4_sc
             nc.vector.tensor_tensor(res[:], gate_win[c][:].indirect(listed(j0, j1)), act[c][h][:, j0 - h * N_TILE : j1 - h * N_TILE], MULT)
             nc.sync.dma_start(out=out[c * P : (c + 1) * P, j0:j1], in_=res[:])
 
-        load_gates(0, 2)
-        for h in range(2):
-            gather_words(1, h)
-            mm4(0, h)
-        load_gates(1, 1)
+        gather_words(1, 0)
+        mm4(0, 0)
         cast_w8()
+        load_gates(0, 2)
+        gather_words(1, 1)
+        mm4(0, 1)
+        load_gates(1, 1)
         quantize_w8()
         gather_words(0, 0)
         mm8(0, 0)

from contextlib import ExitStack

import concourse.mybir as mybir

K, M, T, S = 1024, 256, 2048, 1024
FLOPS = 2 * K * M * S

F32 = mybir.dt.float32
BF16 = mybir.dt.bfloat16
I32 = mybir.dt.int32
U32 = mybir.dt.uint32
U16 = mybir.dt.uint16
U8 = mybir.dt.uint8
FP8X4 = mybir.dt.float8_e4m3fn_x4
FP4X4 = mybir.dt.float4_e2m1fn_x4
GELU = mybir.ActivationFunctionType.Gelu_apprx_tanh
MULT = mybir.AluOpType.mult

P = 128
N_TILE = 512


def tile_list_tabgate_gelu_kernel(tc, tab_words, tab_scales, w8, w4_words, w4_scales, gT, b, offs, out):
    nc = tc.nc
    with ExitStack() as ctx:
        keep = ctx.enter_context(tc.tile_pool(name="keep", bufs=1))
        psum = ctx.enter_context(tc.psum_pool(name="psum", bufs=1))

        offsets = keep.tile([P, S // 16], U16, name="offsets")
        nc.sync.dma_start(offsets[:], offs)

        def listed(j0, j1):
            return offsets[:, j0 // 16 : j1 // 16]

        scale_win = keep.tile([P, T], U8, name="scale_win", align_bytes=64)
        for q in range(4):
            nc.sync.dma_start(out=scale_win[32 * q + 24 : 32 * q + 32, :].bitcast(I32), in_=tab_scales[:, 4 * q : 4 * q + 4, :].bitcast(I32))
            nc.vector.memset(scale_win[32 * q : 32 * q + 24, :].bitcast(I32), 0)

        word_win = [keep.tile([P, T], I32, name=f"word_win{a}", tag=f"window{a}", align_bytes=64) for a in range(2)]
        w8_raw = keep.tile([P, 4, M], F32, name="w8_raw", tag="window2", align_bytes=64)
        w4_plane = keep.tile([P, M], U8, name="w4_plane", align_bytes=64)
        w4_codes = keep.tile([P, 2 * M], U8, name="w4_codes", align_bytes=64)
        bias = keep.tile([P, 2], F32, name="bias")

        def load_words(a):
            nc.sync.dma_start(out=word_win[a][:], in_=tab_words[a].rearrange("p t i -> p (t i)").bitcast(I32))

        def load_w4_scales(q):
            nc.sync.dma_start(out=w4_plane[32 * q : 32 * q + 4, :].bitcast(I32), in_=w4_scales[0, 4 * q : 4 * q + 4, :].bitcast(I32))

        load_words(1)
        load_w4_scales(0)
        load_w4_scales(1)
        nc.sync.dma_start(out=w8_raw[:], in_=w8.rearrange("(p i) n -> p i n", i=4))
        load_w4_scales(2)
        load_w4_scales(3)
        nc.sync.dma_start(out=w4_codes[:].bitcast(I32), in_=w4_words[0].bitcast(I32))
        load_words(0)
        with nc.allow_non_contiguous_dma(reason="one bias value a partition"):
            nc.sync.dma_start(out=bias[:], in_=b.rearrange("(c p) -> p c", p=P))
        gate_win = []

        warm_in = keep.tile([P, 1], F32, name="warm_in")
        warm_out = keep.tile([P, 1], F32, name="warm_out")
        nc.vector.memset(warm_in[:], 0.0)
        nc.scalar.activation(warm_out[:], warm_in[:], GELU)

        picked = keep.tile([P, S], U8, name="picked", align_bytes=64)
        plane = [keep.tile([P, S], U8, name=f"plane{a}", align_bytes=64) for a in range(2)]
        nc.vector.tensor_copy(picked[:], scale_win[:].indirect(offsets[:]))
        nc.scalar.dma_start(out=plane[1][0:100, :].bitcast(I32), in_=picked[28:128, :].bitcast(I32))
        nc.scalar.dma_start(out=plane[0][0:100, :].bitcast(I32), in_=picked[24:124, :].bitcast(I32))

        codes = [[keep.tile([P, N_TILE], U32, name=f"codes{a}_{h}", align_bytes=64) for h in range(2)] for a in range(2)]
        acc = [[psum.tile([P, N_TILE], F32, name=f"acc{c}_{h}") for h in range(2)] for c in range(2)]
        act = [[keep.tile([P, N_TILE], F32, name=f"act{c}_{h}") for h in range(2)] for c in range(2)]
        w8_bf = keep.tile([P, M, 4], BF16, name="w8_bf", align_bytes=64)
        w8_codes = keep.tile([P, M], U32, name="w8_codes", align_bytes=64)
        w8_plane = keep.tile([P, M], U8, name="w8_plane", align_bytes=64)

        def gather_words(a, h, j0=0, j1=N_TILE):
            nc.vector.tensor_copy(codes[a][h][:, j0:j1], word_win[a][:].bitcast(U32).indirect(listed(h * N_TILE + j0, h * N_TILE + j1)))

        def load_gates(c, a):
            gate_win.append(keep.tile([P, T], F32, name=f"gate_win{c}", tag=f"window{a}", align_bytes=64))
            nc.sync.dma_start(out=gate_win[c][:], in_=gT[c * P : (c + 1) * P, :])

        def mm4(c, h):
            nc.tensor.matmul_mx(
                out=acc[c][h][:],
                lhsT=w4_codes[:, 2 * c * P : 2 * (c + 1) * P].bitcast(FP4X4),
                lhsT_scale=w4_plane[:, c * P : (c + 1) * P],
                rhs=codes[1][h][:].bitcast(FP8X4),
                rhs_scale=plane[1][:, h * N_TILE : (h + 1) * N_TILE],
                start=True,
                stop=False,
            )

        def mm8(c, h, j0=0, j1=N_TILE):
            nc.tensor.matmul_mx(
                out=acc[c][h][:, j0:j1],
                lhsT=w8_codes[:, c * P : (c + 1) * P].bitcast(FP8X4),
                lhsT_scale=w8_plane[:, c * P : (c + 1) * P],
                rhs=codes[0][h][:, j0:j1].bitcast(FP8X4),
                rhs_scale=plane[0][:, h * N_TILE + j0 : h * N_TILE + j1],
                start=False,
                stop=(j1 == N_TILE),
            )

        def gelu(c, h, j0=0, j1=N_TILE):
            nc.scalar.activation(act[c][h][:, j0:j1], acc[c][h][:, j0:j1], GELU, bias=bias[:, c : c + 1])

        def cast_w8():
            nc.vector.tensor_copy(out=w8_bf[:], in_=w8_raw[:].rearrange("p i n -> p n i"))

        def quantize_w8():
            nc.vector.quantize_mx(out=w8_codes[:].bitcast(FP8X4), scales=w8_plane[:], in_=w8_bf[:].rearrange("p n i -> p (n i)"))

        def gate(c, j0, j1):
            h = j0 // N_TILE
            res = keep.tile([P, j1 - j0], F32, name=f"res{c}_{j0}")
            nc.vector.tensor_tensor(res[:], gate_win[c][:].indirect(listed(j0, j1)), act[c][h][:, j0 - h * N_TILE : j1 - h * N_TILE], MULT)
            nc.sync.dma_start(out=out[c * P : (c + 1) * P, j0:j1], in_=res[:])

        gather_words(1, 0)
        mm4(0, 0)
        cast_w8()
        load_gates(0, 2)
        gather_words(1, 1)
        mm4(0, 1)
        load_gates(1, 1)
        quantize_w8()
        gather_words(0, 0)
        mm8(0, 0)
        gelu(0, 0)
        for h in range(2):
            mm4(1, h)
        gather_words(0, 1, 0, 256)
        mm8(0, 1, 0, 256)
        gather_words(0, 1, 256, 512)
        mm8(0, 1, 256, 512)
        gelu(0, 1, 0, 256)
        gelu(0, 1, 256, 512)
        for h in range(2):
            mm8(1, h)
            gelu(1, h)
        for c, j0, j1 in [(0, 0, 512), (0, 512, 768), (0, 768, 1024), (1, 0, 512), (1, 512, 896), (1, 896, 1024)]:
            gate(c, j0, j1)
